import numpy as np
import ml_dtypes


def mxq(x, axis, fmt="e4m3"):
    dtype, down = {"e4m3": (ml_dtypes.float8_e4m3fn, 7), "e5m2": (ml_dtypes.float8_e5m2, 14)}[fmt]
    v = np.moveaxis(np.asarray(x, np.float32).astype(ml_dtypes.bfloat16).astype(np.float64), axis, -1)
    blocks = v.reshape(v.shape[:-1] + (-1, 32))
    amax = np.abs(blocks).max(-1, keepdims=True)
    byte = np.maximum(np.where(amax > 0, np.frexp(amax)[1] - 1 + 127, 0) - down, 1)
    scale = np.exp2(byte - 127.0)
    codes = (blocks / scale).astype(np.float32).astype(dtype).astype(np.float64)
    return np.moveaxis((codes * scale).reshape(v.shape), -1, axis)


WIDE = False


def mx_kscale(k):
    if not WIDE:
        return np.ones(k)
    levels = np.array([10, -10, 5, -5, 0])
    if k % 512:
        return np.exp2(np.random.permutation(np.resize(levels, k // 32))).repeat(32)
    a = np.empty((k // 512, 16))
    for p in range(k // 512):
        a[p, :8] = np.random.permutation(np.resize(levels, 8))
        for g in range(8):
            far = levels[np.abs(levels - a[p, g]) >= 10]
            a[p, g + 8] = far[np.random.randint(len(far))]
    return np.exp2(a.ravel()).repeat(32)


BF16 = ml_dtypes.bfloat16


def bf(x):
    return np.asarray(x, np.float32).astype(BF16)


def f64(x):
    return np.asarray(x).astype(np.float64)

E4M3FN = np.array([(-1.0 if i & 128 else 1.0) * ((1.0 + (i & 7) / 8.0) * 2.0 ** (((i >> 3) & 15) - 7) if i & 120 else (i & 7) * 2.0 ** -9) for i in range(256)])


def e4m3fn_bytes(y):
    return np.clip(np.asarray(y, np.float64), -448.0, 448.0).astype(np.float32).astype(ml_dtypes.float8_e4m3fn).view(np.uint8)


def e4m3fn_values(b):
    return E4M3FN[b]


V, U, I = 512, 2048, 1536
E4M3_MAX = 448.0


def setup_inputs():
    s, t = mx_kscale(U), mx_kscale(I)
    a = np.random.standard_normal((U, I)) / np.sqrt(U) / s[:, None]
    b = np.random.standard_normal((I, U)) / np.sqrt(I) / t[:, None]
    a_scale = (np.abs(a).max(axis=1, keepdims=True) / E4M3_MAX).astype(np.float32)
    b_scale = (np.abs(b).max(axis=1, keepdims=True) / E4M3_MAX).astype(np.float32)
    return {"ranks": bf(np.random.standard_normal((U, V)) * s[:, None]),
            "A_bytes": e4m3fn_bytes(a / f64(a_scale)),
            "A_scale": a_scale,
            "damp_items": bf((0.75 + 0.2 * np.random.random(I)) * t),
            "tele_items": bf(0.4 * np.random.standard_normal(I) * t),
            "B_bytes": e4m3fn_bytes(b / f64(b_scale)),
            "B_scale": b_scale,
            "damp_users": bf(0.75 + 0.2 * np.random.random(U)),
            "tele_users": bf(0.4 * np.random.standard_normal((U, V)))}


def reference(ranks, A_bytes, A_scale, damp_items, tele_items, B_bytes, B_scale, damp_users, tele_users):
    a = e4m3fn_values(A_bytes) * np.repeat(f64(A_scale), I, axis=1)
    b = e4m3fn_values(B_bytes) * np.repeat(f64(B_scale), U, axis=1)
    y = mxq(a, 0, "e4m3").T @ mxq(f64(ranks), 0, "e4m3")
    y = f64(damp_items)[:, None] * y + f64(tele_items)[:, None]
    z = mxq(b, 0, "e4m3").T @ mxq(y, 0, "e4m3")
    return f64(damp_users)[:, None] * z + f64(tele_users)

from contextlib import ExitStack

import concourse.mybir as mybir
from concourse.masks import make_identity

V, U, I = 512, 2048, 1536
FLOPS = 2 * 2 * V * U * I

F32 = mybir.dt.float32
BF16 = mybir.dt.bfloat16
U32 = mybir.dt.uint32
U8 = mybir.dt.uint8
FP8 = mybir.dt.float8_e4m3fn
FP8X4 = mybir.dt.float8_e4m3fn_x4
ACT = mybir.ActivationFunctionType
ALU = mybir.AluOpType

P = 128
PACK = 4
W = 512
ORDER = """
iV:R0 wS:A00 q:R0 iV:R1 wS:A01 iV:A00 c:0 q:R1 q:A00 wS:A02 iV:R2 mm:A00:0 mm:A00:1 mm:A00:2 mm:A00:3 iV:A01
wS:A03 q:R2 q:A01 iV:A02 wS:A10 mm:A01:0 mm:A01:1 mm:A01:2 mm:A01:3 iV:R3 wS:A11 q:A02 q:R3 mm:A02:0 iV:A03
mm:A02:1 mm:A02:2 mm:A02:3 wS:A12 iV:A10 q:A03 wS:A13 q:A10 mm:A03:0 iV:A11 mm:A03:1 mm:A03:2 mm:A03:3
mm:A10:0 mm:A10:1 iV:A12 y:0:0 mm:A10:2 y:0:1 mm:A10:3 y:0:2 q:A11 y:0:3 q:A12 mm:A11:0 wS:A20 iV:A13 mm:A11:1
mm:A11:2 mm:A11:3 mm:A12:0 mm:A12:1 iV:Y0 mm:A12:2 mm:A12:3 wS:A21 q:A13 q:Y0 mm:A13:0 iV:A20 mm:A13:1
mm:A13:2 mm:A13:3 wS:A22 iV:A21 q:A20 y:1:0 q:A21 y:1:1 mm:A20:0 iV:A22 mm:A20:1 y:1:2 mm:A20:2 mm:A20:3 y:1:3
mm:A21:0 mm:A21:1 wS:A23 wV:B30 mm:A21:2 mm:A21:3 q:A22 iV:Y1 mm:A22:0 wS:B00 mm:A22:1 mm:A22:2 mm:A22:3
iV:A23 q:Y1 wS:B01 q:A23 iV:B00 mm:A23:0 mm:A23:1 mm:A23:2 y:2:0 mm:A23:3 iV:B01 y:2:1 y:2:2 q:B00 y:2:3 q:B01
mm:B00:0 wS:B02 iV:Y2 mm:B00:1 mm:B00:2 mm:B00:3 mm:B01:0 iV:B30 mm:B01:1 mm:B01:2 mm:B01:3 wS:B10 q:Y2 iV:B02
wS:B11 q:B30 q:B02 iV:B10 mm:B02:0 mm:B02:1 mm:B02:2 wS:B12 mm:B02:3 o:0:0 o:0:2 o:0:3 o:0:1 wS:B20 q:B10
iV:B12 mm:B10:0 mm:B10:1 mm:B10:2 mm:B10:3 iV:B11 wS:B21 q:B12 q:B11 wS:B22 iV:B20 mm:B11:0 mm:B11:1 mm:B11:2
mm:B11:3 iV:B21 mm:B12:0 mm:B12:1 mm:B12:2 wS:B31 mm:B12:3 o:1:1 o:1:2 o:1:3 o:1:0 wS:B32 q:B20 q:B21 mm:B20:0
iV:B22 mm:B20:1 mm:B20:2 mm:B20:3 iS:B32 mm:B21:0 iV:B31 mm:B21:1 mm:B21:2 mm:B21:3 mm:B30:0 q:B22 mm:B30:1
mm:B30:2 q:B31 mm:B22:0 q:B32 mm:B22:1 mm:B22:2 o:2:0 mm:B22:3 mm:B31:0 o:2:2 mm:B30:3 mm:B31:1 o:2:3 mm:B31:2
mm:B31:3 o:2:1 mm:B32:0 mm:B32:1 mm:B32:2 o:3:0 mm:B32:3 o:3:2 o:3:1 o:3:3
""".split()
LOADS = "sA R0 A00 R1 A01 small R2 A02 R3 A03 A10 A11 A12 A13 A20 A21 A22 A23 B00 B01 B02 T0 B10 B11 B12 T1 B20 B21 B22 T2 B30 B31 B32 T3".split()
SLOTS = {"wide": 7, "grouped": 4, "acc": 7, "weave": 0, "result": 6}


def tile_signed_bipartite_rank_step_d5_kernel(
    tc, ranks, A_bytes, A_scale, damp_items, tele_items, B_bytes, B_scale, damp_users, tele_users, out
):
    nc = tc.nc
    with ExitStack() as ctx:
        keep = ctx.enter_context(tc.tile_pool(name="keep", bufs=1))
        psum = ctx.enter_context(tc.psum_pool(name="psum", bufs=1))
        ctx.enter_context(tc.manual_schedule())

        free = {kind: list(range(n)) for kind, n in SLOTS.items()}
        held = {}

        def take(kind, key, shape, dtype):
            slot = free[kind].pop(0)
            if kind in ("acc", "weave"):
                t = psum.tile(shape, dtype, name="%s%d" % (kind, slot), tag="%s%d" % (kind, slot))
            else:
                t = keep.tile(shape, dtype, name="%s%d" % (kind, slot), tag="%s%d" % (kind, slot), align_bytes=64)
            held[(kind, key)] = (slot, t)
            return t

        def get(kind, key):
            return held[(kind, key)][1]

        def give(kind, key):
            free[kind].append(held.pop((kind, key))[0])

        ident32 = keep.tile([P, P], F32, name="ident32")
        ident = keep.tile([P, P], BF16, name="ident")
        damp_rows = keep.tile([P, P], BF16, name="damp_rows")
        make_identity(nc, ident32[:])
        nc.gpsimd.memset(damp_rows[:], 0.0)
        nc.scalar.activation(out=ident[:], in_=ident32[:], func=ACT.Copy)

        scale = {
            "A": keep.tile([P, U // W, PACK], F32, name="a_scale"),
            "B": keep.tile([P, I // W, PACK], F32, name="b_scale"),
        }
        damp_i16 = keep.tile([P, I // W, PACK], BF16, name="damp_i16")
        tele_i = keep.tile([P, I // W, PACK], BF16, name="tele_i")
        damp_i = keep.tile([P, I // W, PACK], F32, name="damp_i")
        damp_u = keep.tile([P, U // P], F32, name="damp_u")
        raw = {}
        for name in LOADS:
            if name == "sA":
                nc.sync.dma_start(out=scale["A"][:], in_=A_scale.rearrange("(g p t) o -> p g (t o)", p=P, t=PACK))
            elif name == "small":
                nc.sync.dma_start(out=scale["B"][:], in_=B_scale.rearrange("(g p t) o -> p g (t o)", p=P, t=PACK))
                nc.sync.dma_start(out=damp_i16[:], in_=damp_items.rearrange("(g p t) -> p g t", p=P, t=PACK))
                nc.sync.dma_start(out=tele_i[:], in_=tele_items.rearrange("(g p t) -> p g t", p=P, t=PACK))
                nc.sync.dma_start(out=damp_rows[: U // P, :], in_=damp_users.rearrange("(j p) -> j p", p=P))
            elif name[0] == "R":
                g = int(name[1])
                raw[name] = keep.tile([P, PACK, W], BF16, name="ranks_" + name, align_bytes=64)
                nc.sync.dma_start(out=raw[name][:], in_=ranks[g * W : (g + 1) * W, :].rearrange("(p t) v -> p t v", t=PACK))
            elif name[0] == "T":
                c = int(name[1])
                raw[name] = keep.tile([P, PACK, V], BF16, name="tele_" + name, align_bytes=64)
                nc.sync.dma_start(out=raw[name][:], in_=tele_users[c * W : (c + 1) * W, :].rearrange("(j p) v -> p j v", p=P))
            else:
                c, g = int(name[1]), int(name[2])
                src = A_bytes if name[0] == "A" else B_bytes
                raw[name] = keep.tile([P, PACK, W], U8, name="fp8_" + name, align_bytes=64)
                nc.sync.dma_start(
                    out=raw[name][:],
                    in_=src[g * W : (g + 1) * W, c * W : (c + 1) * W].rearrange("(p t) n -> p t n", t=PACK),
                )

        codes = {}
        scales = {}

        def planes(unit):
            return raw[unit] if unit[0] == "R" else get("wide", unit)

        for step in ORDER:
            kind, unit = step.split(":")[0], step.split(":")[1]
            j = int(step.split(":")[2]) if step.count(":") == 2 else 0
            if kind == "c":
                nc.vector.tensor_copy(out=damp_i[:], in_=damp_i16[:])
                turned = take("acc", "damp", [P, P], BF16)
                nc.tensor.transpose(turned[:], damp_rows[:], ident[:])
                nc.vector.tensor_copy(out=damp_u[:], in_=turned[:, : U // P])
                give("acc", "damp")
            elif kind in ("wS", "wV"):
                wide = take("wide", unit, [P, PACK, W], BF16)
                g = int(unit[2])
                for t in range(PACK):
                    col = scale[unit[0]][:, g, t : t + 1]
                    if kind == "wS":
                        nc.scalar.activation(out=wide[:, t, :], in_=raw[unit][:, t, :].bitcast(FP8), func=ACT.Copy, scale=col)
                    else:
                        nc.vector.tensor_scalar(
                            out=wide[:, t, :], in0=raw[unit][:, t, :].bitcast(FP8), scalar1=col, scalar2=None, op0=ALU.mult
                        )
            elif kind == "y":
                g = int(unit)
                if j == 0:
                    take("wide", "Y" + unit, [P, PACK, W], BF16)
                nc.scalar.activation(
                    out=get("wide", "Y" + unit)[:, j, :],
                    in_=get("acc", ("A" + unit, j))[:],
                    func=ACT.Identity,
                    scale=damp_i[:, g, j : j + 1],
                    bias=tele_i[:, g, j : j + 1],
                )
                give("acc", ("A" + unit, j))
            elif kind in ("iV", "iS"):
                grouped = take("grouped", unit, [P, PACK * W], BF16)
                src = planes(unit)
                if unit[0] == "A":
                    dst = grouped[:].rearrange("p (s m e t) -> p m s e t", s=PACK, e=2, t=PACK)
                    src = src[:].rearrange("p t (m e s) -> p m s e t", s=PACK, e=2)
                else:
                    dst = grouped[:].rearrange("p (c i t) -> p c t i", i=4, t=PACK)
                    src = src[:].rearrange("p t (c i) -> p c t i", i=4)
                if kind == "iV":
                    nc.vector.tensor_copy(out=dst, in_=src)
                else:
                    nc.scalar.copy(out=dst, in_=src)
                if unit[0] != "R":
                    give("wide", unit)
            elif kind == "pm":
                bank = take("weave", (unit, j), [P, 2 * W], BF16)
                src = planes(unit)
                for k in range(2):
                    q = 2 * j + k
                    if unit[0] == "A":
                        rhs = src[:].rearrange("p t (m s) -> p s m t", s=PACK)[:, q, :, :]
                    else:
                        rhs = src[:, :, q * P : (q + 1) * P].rearrange("p t c -> p c t")
                    nc.tensor.matmul(
                        bank[:, k * W : (k + 1) * W].rearrange("p (c t) -> p c t", t=PACK), lhsT=ident[:], rhs=rhs, start=True, stop=True
                    )
                if j == 1 and unit[0] != "R":
                    give("wide", unit)
            elif kind == "pc":
                if j == 0:
                    take("grouped", unit, [P, PACK * W], BF16)
                nc.scalar.copy(out=get("grouped", unit)[:, j * 2 * W : (j + 1) * 2 * W], in_=get("weave", (unit, j))[:])
                give("weave", (unit, j))
            elif kind == "q":
                codes[unit] = keep.tile([P, W], U32, name="codes_" + unit, align_bytes=64)
                scales[unit] = keep.tile([P, W], U8, name="scales_" + unit, align_bytes=64)
                nc.vector.quantize_mx(out=codes[unit][:].bitcast(FP8X4), scales=scales[unit][:], in_=get("grouped", unit)[:])
                give("grouped", unit)
            elif kind == "mm":
                g = int(unit[2])
                last = 3 if unit[0] == "A" else 2
                other = ("R" if unit[0] == "A" else "Y") + unit[2]
                if g == 0:
                    take("acc", (unit[:2], j), [P, V], F32)
                nc.tensor.matmul_mx(
                    out=get("acc", (unit[:2], j))[:],
                    lhsT=codes[unit][:, j * P : (j + 1) * P].bitcast(FP8X4),
                    lhsT_scale=scales[unit][:, j * P : (j + 1) * P],
                    rhs=codes[other][:].bitcast(FP8X4),
                    rhs_scale=scales[other][:],
                    start=(g == 0),
                    stop=(g == last),
                )
            else:
                c = int(unit)
                row = c * PACK + j
                result = take("result", row, [P, V], F32)
                nc.vector.scalar_tensor_tensor(
                    out=result[:],
                    in0=get("acc", ("B" + unit, j))[:],
                    scalar=damp_u[:, row : row + 1],
                    in1=raw["T" + unit][:, j, :],
                    op0=ALU.mult,
                    op1=ALU.add,
                )
                give("acc", ("B" + unit, j))
                nc.sync.dma_start(out=out[row * P : (row + 1) * P, :], in_=result[:])
                give("result", row)
